import numpy as np
CORES = [0,1,2,3,4,5,6,7,8,9,10,11,12,13,14,15,16,17,18,19,20,21,22,23,24,25,26,27,28,29,30,31,128,129,130,131,132,133,134,135,136,137,138,139,140,141,142,143,144,145,146,147,148,149,150,151,152,153,154,155,156,157,158,159]
N = 64
TOK, D = 32, 512
ROUTE = [[[20,46],[0,9],[20,22],[17,35],[0,6],[20,54],[7,13],[8,13],[8,15],[49,51],[51,55],[58,62],[43,45],[33,37],[26,27],[10,32],[11,13],[21,56],[28,63],[45,47],[35,40],[1,3],[5,31],[40,43],[4,51],[50,54],[36,49],[7,56],[45,46],[0,49],[22,62],[54,58]],[[17,23],[11,13],[13,22],[3,17],[3,57],[8,17],[7,21],[9,49],[59,61],[11,50],[56,59],[12,13],[14,31],[12,13],[25,60],[37,39],[34,37],[56,58],[2,5],[9,14],[23,39],[12,23],[57,61],[48,54],[57,63],[51,53],[14,15],[25,61],[58,59],[27,30],[4,11],[24,27]],[[10,41],[19,20],[52,53],[12,53],[20,23],[8,14],[12,23],[19,23],[42,43],[11,14],[28,31],[9,33],[40,47],[8,45],[11,13],[18,19],[48,52],[9,40],[33,34],[46,56],[19,20],[55,62],[45,46],[48,49],[48,49],[24,27],[6,31],[28,53],[12,41],[22,37],[53,54],[2,5]],[[33,38],[33,37],[8,9],[13,40],[11,15],[27,28],[61,63],[11,14],[25,62],[49,52],[59,63],[46,47],[50,54],[18,19],[46,58],[11,17],[45,47],[48,51],[5,7],[57,62],[1,51],[15,56],[32,33],[2,4],[49,54],[35,42],[33,35],[36,38],[0,36],[33,44],[48,51],[8,31]],[[0,4],[4,5],[26,29],[50,54],[5,32],[0,4],[43,44],[0,6],[29,43],[8,54],[5,6],[9,10],[56,58],[26,42],[56,62],[5,28],[18,32],[16,17],[11,12],[21,56],[12,13],[15,21],[50,52],[6,47],[11,28],[8,15],[16,22],[12,37],[15,52],[36,39],[2,10],[56,61]],[[56,61],[4,22],[18,21],[58,60],[6,36],[26,29],[12,63],[25,29],[18,43],[19,21],[29,31],[27,43],[25,49],[15,47],[20,21],[18,22],[59,62],[58,59],[40,46],[33,36],[22,23],[52,53],[5,47],[2,48],[26,51],[19,21],[56,63],[41,46],[12,51],[28,58],[28,29],[21,22]],[[3,45],[21,23],[8,13],[8,52],[0,2],[8,14],[0,15],[17,18],[9,12],[9,49],[33,61],[30,52],[29,54],[25,28],[18,23],[11,13],[16,19],[20,32],[37,58],[5,20],[2,29],[22,36],[0,29],[23,50],[35,36],[17,19],[48,51],[34,38],[19,33],[18,19],[49,50],[37,53]],[[27,63],[34,36],[10,13],[32,36],[50,53],[26,40],[49,55],[26,29],[40,41],[6,45],[0,5],[24,25],[17,23],[57,59],[59,62],[44,45],[40,43],[48,55],[20,22],[5,39],[11,62],[3,5],[3,4],[40,46],[24,31],[13,14],[44,62],[59,62],[3,38],[16,20],[49,54],[58,61]],[[17,19],[26,35],[34,37],[16,18],[35,36],[38,62],[19,23],[13,15],[2,8],[0,2],[43,63],[26,38],[41,47],[28,49],[7,60],[10,16],[9,14],[30,31],[9,29],[59,62],[49,63],[9,46],[35,49],[16,47],[13,15],[27,28],[36,39],[60,61],[4,48],[50,53],[26,30],[55,59]],[[23,58],[45,51],[21,56],[43,45],[57,59],[0,7],[32,34],[33,34],[17,63],[10,57],[5,7],[58,59],[49,54],[25,29],[39,48],[17,57],[56,61],[28,30],[32,36],[15,52],[43,47],[32,34],[6,54],[10,11],[34,35],[21,22],[44,53],[25,27],[36,40],[13,50],[17,24],[38,39]],[[12,15],[4,6],[34,42],[14,49],[1,6],[11,12],[16,22],[18,60],[56,63],[32,36],[13,14],[49,58],[49,52],[24,30],[48,55],[17,45],[4,29],[36,55],[9,15],[34,48],[18,32],[12,41],[49,53],[4,6],[21,60],[3,32],[17,22],[5,6],[14,50],[12,48],[0,7],[38,39]],[[4,61],[14,51],[20,23],[58,63],[25,47],[42,47],[57,62],[16,22],[23,62],[45,51],[9,57],[9,13],[7,46],[11,15],[9,14],[57,59],[20,28],[7,61],[52,55],[1,33],[50,53],[39,50],[33,37],[6,49],[8,9],[20,22],[7,62],[56,57],[16,19],[8,9],[17,20],[24,27]],[[15,52],[19,22],[4,47],[57,63],[9,14],[41,46],[27,28],[10,12],[1,32],[7,43],[44,45],[56,60],[0,5],[57,63],[44,46],[9,30],[54,55],[45,54],[41,47],[34,38],[18,20],[41,45],[9,13],[13,55],[40,47],[56,59],[13,40],[8,55],[58,62],[43,62],[20,50],[10,12]],[[17,20],[49,54],[56,58],[11,45],[10,12],[18,19],[34,38],[44,46],[27,38],[0,54],[8,52],[3,6],[52,55],[20,23],[46,56],[56,60],[1,2],[3,7],[38,40],[13,31],[50,58],[5,55],[4,7],[16,18],[29,31],[56,62],[50,61],[9,42],[34,39],[51,55],[42,46],[2,24]],[[33,50],[8,22],[50,51],[19,20],[1,62],[57,60],[43,54],[3,5],[2,54],[21,23],[1,2],[27,29],[5,61],[23,44],[56,60],[20,22],[45,49],[22,45],[46,47],[10,11],[2,10],[25,36],[2,52],[3,6],[40,47],[58,60],[28,59],[8,12],[34,36],[24,26],[40,44],[54,62]],[[58,61],[49,53],[16,17],[59,62],[43,49],[34,36],[19,21],[12,18],[15,58],[26,31],[12,15],[18,20],[40,42],[6,45],[17,18],[18,21],[39,45],[29,31],[15,22],[20,29],[13,14],[29,30],[18,19],[53,54],[41,62],[32,34],[3,4],[46,47],[54,55],[25,30],[3,6],[18,29]],[[51,53],[9,12],[32,36],[25,30],[4,7],[16,21],[9,35],[19,46],[11,15],[14,15],[6,7],[16,21],[2,7],[46,47],[47,57],[35,55],[10,13],[45,50],[44,59],[4,9],[23,28],[21,23],[3,7],[49,52],[49,51],[23,63],[5,7],[6,52],[17,21],[48,55],[38,43],[22,54]],[[25,30],[57,59],[27,31],[45,55],[34,39],[25,26],[11,26],[3,7],[10,13],[58,59],[16,22],[37,56],[6,38],[25,63],[16,19],[24,30],[6,43],[42,44],[41,44],[16,22],[16,23],[42,43],[1,44],[35,38],[24,32],[34,37],[9,54],[13,49],[27,53],[25,26],[12,14],[32,47]],[[4,7],[46,47],[30,46],[0,26],[18,20],[20,22],[29,31],[11,17],[17,56],[10,11],[35,36],[40,47],[26,29],[25,43],[36,39],[0,53],[19,25],[56,59],[41,44],[16,19],[18,20],[4,7],[9,13],[41,47],[35,36],[49,52],[48,54],[0,7],[19,21],[20,21],[48,50],[61,63]],[[17,19],[20,53],[4,9],[8,15],[0,26],[49,52],[30,58],[62,63],[38,39],[16,33],[40,50],[2,10],[20,32],[42,47],[10,11],[56,57],[33,36],[51,55],[8,14],[40,46],[16,21],[31,55],[12,14],[48,50],[11,14],[10,14],[47,55],[33,38],[17,42],[3,58],[18,23],[37,41]],[[27,28],[10,14],[57,61],[21,22],[21,23],[40,41],[11,15],[27,28],[21,63],[33,42],[41,46],[7,45],[53,59],[17,31],[3,28],[40,44],[50,52],[1,22],[47,60],[15,33],[43,44],[16,17],[11,60],[17,53],[29,31],[26,54],[1,4],[26,30],[36,39],[11,48],[25,43],[22,23]],[[59,62],[16,52],[8,13],[15,57],[12,54],[42,43],[50,52],[46,58],[58,59],[8,13],[19,20],[1,3],[0,5],[34,36],[3,4],[1,5],[42,59],[16,39],[6,35],[56,61],[7,27],[53,55],[18,22],[2,3],[11,52],[26,28],[50,51],[9,27],[1,53],[42,52],[26,28],[19,39]],[[10,58],[7,49],[31,46],[39,54],[19,20],[12,13],[8,13],[29,30],[53,59],[18,34],[15,42],[8,15],[33,37],[30,34],[44,45],[43,47],[12,14],[17,18],[58,60],[8,15],[52,53],[40,44],[0,4],[33,34],[49,51],[30,35],[52,53],[21,22],[52,53],[44,46],[1,9],[19,41]],[[0,15],[1,9],[12,14],[48,50],[24,28],[2,3],[15,54],[1,36],[1,6],[16,19],[21,25],[52,55],[10,15],[60,62],[41,47],[18,20],[0,6],[20,60],[28,48],[15,56],[25,32],[16,25],[3,28],[19,20],[16,18],[38,41],[22,47],[27,39],[56,62],[27,31],[33,49],[26,28]],[[40,41],[42,45],[42,46],[10,13],[43,54],[49,53],[36,38],[12,44],[50,55],[5,7],[26,27],[16,23],[61,62],[58,61],[40,41],[5,18],[21,44],[1,60],[27,28],[16,34],[56,63],[22,34],[47,52],[49,52],[17,40],[32,36],[1,31],[14,38],[24,35],[16,20],[25,60],[41,62]],[[0,35],[5,26],[25,31],[4,57],[46,47],[26,29],[53,54],[57,59],[5,14],[48,52],[24,27],[27,30],[8,55],[32,40],[18,39],[53,54],[45,47],[25,35],[35,58],[28,58],[48,50],[21,23],[22,63],[5,40],[34,36],[17,46],[21,56],[18,22],[28,44],[41,43],[24,50],[57,63]],[[18,63],[1,7],[32,34],[23,60],[7,33],[13,31],[16,20],[6,18],[12,15],[9,11],[45,49],[8,43],[28,60],[34,37],[29,55],[27,31],[42,63],[4,5],[24,39],[23,27],[58,62],[34,35],[56,58],[2,3],[19,23],[11,41],[1,7],[29,57],[24,26],[33,42],[39,57],[10,14]],[[51,54],[16,38],[19,46],[33,49],[42,46],[35,39],[32,53],[2,6],[12,42],[16,57],[37,39],[10,13],[25,28],[46,61],[27,56],[1,39],[32,33],[10,15],[52,53],[57,60],[54,55],[1,34],[9,14],[28,59],[57,60],[50,54],[41,47],[58,63],[48,53],[2,29],[6,7],[49,55]],[[48,55],[4,7],[30,31],[9,10],[44,45],[10,15],[59,63],[23,39],[38,52],[29,37],[46,48],[12,61],[16,17],[6,10],[13,15],[0,32],[33,38],[37,38],[18,63],[10,57],[8,17],[10,17],[10,12],[25,31],[40,44],[7,61],[24,28],[51,61],[0,4],[4,7],[33,37],[24,29]],[[49,50],[18,44],[33,46],[18,20],[16,61],[5,35],[27,29],[62,63],[13,27],[32,40],[52,61],[17,18],[23,36],[49,52],[3,23],[18,19],[18,23],[35,39],[42,45],[35,36],[22,32],[13,48],[6,7],[21,22],[16,36],[2,6],[30,31],[1,41],[18,20],[4,48],[52,53],[19,53]],[[37,54],[57,60],[32,56],[34,35],[15,17],[20,62],[48,53],[36,39],[33,37],[4,63],[42,46],[40,44],[25,42],[41,43],[48,55],[10,53],[29,30],[50,54],[8,61],[2,5],[32,37],[19,39],[49,50],[4,61],[57,62],[58,61],[18,22],[52,53],[12,15],[9,14],[36,39],[37,51]],[[61,63],[43,44],[53,61],[24,26],[0,54],[35,39],[25,57],[11,46],[52,56],[14,26],[38,39],[6,23],[0,45],[10,12],[45,60],[9,15],[9,10],[11,34],[18,20],[58,62],[30,47],[14,21],[24,54],[10,14],[24,26],[25,53],[37,38],[49,53],[50,53],[2,33],[14,45],[3,4]],[[25,26],[8,9],[26,62],[6,40],[24,40],[60,63],[48,51],[25,28],[29,59],[20,36],[37,63],[35,44],[56,57],[8,43],[30,31],[12,40],[31,62],[48,50],[14,55],[10,20],[31,55],[56,58],[20,46],[29,31],[24,26],[12,45],[33,34],[8,10],[48,50],[59,60],[4,13],[1,21]],[[11,14],[16,23],[28,30],[3,4],[1,2],[0,63],[48,51],[36,37],[44,52],[14,57],[0,6],[56,59],[45,59],[15,59],[12,15],[45,47],[24,49],[25,28],[10,11],[6,43],[0,3],[9,13],[16,19],[26,27],[52,58],[56,61],[56,59],[37,59],[22,23],[31,43],[31,59],[22,59]],[[36,54],[44,45],[17,23],[11,13],[1,19],[1,5],[37,39],[16,39],[7,24],[2,35],[51,53],[8,10],[34,62],[45,60],[1,59],[52,53],[20,22],[27,33],[37,58],[39,48],[33,35],[19,48],[33,35],[24,26],[40,41],[42,45],[19,23],[13,48],[9,14],[34,55],[17,19],[30,40]],[[0,7],[8,10],[57,59],[16,38],[36,48],[48,54],[2,14],[24,29],[34,37],[25,32],[40,42],[59,61],[20,57],[24,29],[24,25],[30,32],[50,54],[56,61],[25,27],[48,55],[23,36],[8,10],[45,46],[26,32],[48,51],[38,46],[11,33],[28,31],[26,53],[24,29],[33,39],[10,14]],[[43,45],[19,23],[33,39],[25,27],[28,30],[54,62],[16,17],[33,37],[24,26],[11,13],[26,29],[57,62],[31,50],[34,35],[34,38],[42,45],[50,54],[21,22],[41,44],[51,55],[27,30],[48,49],[0,58],[16,62],[23,48],[18,21],[32,38],[2,3],[37,38],[8,40],[0,8],[54,55]],[[18,19],[20,46],[37,39],[10,46],[27,30],[24,29],[9,52],[22,33],[0,3],[61,63],[2,26],[27,31],[33,34],[44,45],[13,14],[16,18],[11,15],[8,13],[13,20],[0,14],[28,60],[8,40],[17,18],[24,54],[25,31],[25,27],[37,62],[9,12],[14,17],[41,56],[26,31],[3,22]],[[5,24],[38,50],[16,22],[54,55],[0,57],[19,20],[42,44],[53,55],[27,38],[42,43],[36,37],[48,53],[47,58],[20,22],[28,29],[22,38],[1,63],[56,62],[44,45],[55,58],[15,54],[24,29],[28,29],[56,62],[14,48],[49,60],[14,42],[9,15],[60,61],[22,62],[32,34],[40,44]],[[40,43],[1,5],[51,53],[8,60],[18,20],[41,43],[26,28],[12,13],[13,36],[22,23],[8,13],[22,58],[4,47],[16,52],[11,12],[40,42],[43,59],[4,6],[29,31],[25,62],[29,30],[37,60],[51,53],[9,11],[33,34],[2,12],[54,62],[22,56],[49,50],[58,60],[44,45],[17,23]],[[46,47],[17,19],[57,59],[0,5],[18,23],[51,54],[18,30],[57,63],[35,39],[18,19],[45,46],[9,14],[11,15],[56,61],[9,14],[16,21],[17,51],[8,11],[1,2],[60,61],[46,55],[48,50],[20,21],[40,60],[50,53],[0,5],[52,53],[1,3],[18,23],[48,53],[40,47],[18,21]],[[12,38],[25,36],[0,5],[56,60],[24,63],[3,37],[48,59],[20,36],[38,58],[8,15],[1,3],[46,54],[11,57],[8,13],[55,63],[41,42],[4,21],[1,3],[17,22],[61,62],[41,42],[13,14],[4,6],[34,35],[21,23],[58,62],[0,5],[26,29],[5,57],[18,20],[44,46],[45,47]],[[0,37],[12,14],[5,39],[4,49],[9,12],[32,33],[2,6],[19,20],[2,30],[58,63],[56,58],[40,47],[42,47],[16,21],[1,4],[7,34],[54,60],[11,56],[1,53],[16,50],[12,50],[34,37],[2,12],[18,19],[6,7],[0,15],[40,41],[35,62],[57,63],[4,58],[59,60],[1,6]],[[10,14],[0,37],[59,63],[55,61],[10,15],[13,22],[33,34],[8,14],[37,55],[38,55],[13,25],[51,58],[42,43],[28,29],[13,36],[50,51],[35,48],[5,41],[5,11],[18,23],[42,47],[21,23],[12,38],[19,21],[15,40],[50,54],[16,20],[39,47],[7,55],[8,15],[12,44],[51,54]],[[44,59],[17,20],[12,26],[6,54],[24,54],[58,59],[59,62],[2,3],[9,11],[41,43],[0,44],[57,61],[42,47],[16,23],[36,63],[33,36],[4,7],[43,44],[2,3],[13,15],[42,44],[13,14],[48,49],[5,7],[4,52],[11,21],[17,20],[12,13],[35,40],[25,33],[9,11],[10,48]],[[48,53],[27,28],[26,54],[48,51],[26,30],[56,61],[41,42],[40,46],[58,62],[33,37],[25,29],[17,21],[19,23],[16,19],[18,29],[13,46],[58,59],[24,26],[38,55],[40,44],[10,15],[11,47],[24,25],[2,5],[15,48],[6,7],[10,15],[40,45],[44,46],[42,45],[39,56],[25,28]],[[1,5],[32,33],[1,7],[20,23],[5,57],[26,28],[14,31],[26,51],[18,35],[32,33],[14,38],[50,54],[16,55],[32,39],[1,2],[2,7],[11,17],[33,39],[11,15],[13,19],[11,43],[58,63],[30,35],[60,62],[53,54],[52,54],[12,62],[20,30],[0,29],[1,59],[35,36],[2,37]],[[27,28],[21,24],[4,7],[5,54],[2,6],[47,63],[52,54],[4,7],[4,49],[51,53],[44,45],[51,61],[49,50],[5,7],[0,4],[49,50],[36,45],[25,30],[24,52],[35,36],[42,43],[50,54],[59,60],[33,42],[28,40],[25,31],[51,52],[1,62],[2,20],[19,20],[35,37],[27,54]],[[15,26],[3,7],[10,12],[17,29],[10,26],[20,28],[52,53],[4,6],[31,63],[21,47],[21,40],[49,53],[4,41],[6,51],[56,59],[41,47],[18,22],[8,9],[11,21],[44,46],[2,3],[0,6],[40,43],[48,55],[3,7],[28,48],[16,19],[7,23],[33,38],[4,42],[31,55],[4,5]],[[46,51],[17,39],[3,44],[40,41],[52,55],[42,45],[48,59],[41,43],[21,23],[9,15],[10,57],[51,52],[50,51],[18,23],[2,18],[26,27],[0,5],[36,39],[36,38],[32,35],[24,29],[46,47],[26,43],[42,46],[3,7],[5,30],[9,10],[5,38],[2,58],[51,54],[40,46],[59,63]],[[39,42],[14,42],[45,46],[39,57],[49,55],[36,52],[28,59],[24,29],[56,57],[33,46],[0,27],[30,44],[40,43],[4,41],[8,23],[21,40],[16,47],[4,50],[42,47],[26,31],[41,44],[50,53],[41,43],[25,31],[8,10],[26,63],[18,24],[56,60],[5,6],[11,59],[24,27],[48,52]],[[35,39],[36,38],[12,14],[4,9],[8,14],[33,34],[2,8],[16,48],[56,60],[30,33],[9,11],[24,28],[26,55],[36,38],[8,11],[19,20],[27,30],[2,36],[37,38],[45,46],[8,52],[1,10],[18,19],[11,57],[16,18],[22,42],[6,48],[19,58],[2,4],[11,23],[28,61],[4,55]],[[56,59],[6,34],[3,36],[30,57],[48,51],[51,54],[42,54],[48,54],[55,56],[37,38],[48,51],[50,54],[49,51],[19,51],[42,62],[12,15],[34,52],[57,63],[57,59],[25,46],[44,46],[51,60],[26,27],[36,39],[34,38],[14,22],[57,59],[18,57],[57,60],[57,62],[56,61],[19,22]],[[17,20],[21,52],[29,31],[57,60],[58,63],[12,25],[16,47],[16,36],[8,36],[4,31],[11,13],[4,18],[57,58],[10,14],[42,46],[7,25],[16,19],[44,57],[1,2],[10,14],[10,11],[43,44],[31,62],[11,37],[32,33],[53,56],[16,19],[4,24],[26,29],[19,42],[24,30],[2,3]],[[6,37],[0,1],[5,8],[16,54],[2,6],[57,58],[12,27],[41,42],[56,63],[45,46],[43,45],[12,20],[9,11],[56,58],[15,28],[43,50],[3,28],[5,14],[6,33],[30,60],[13,14],[56,59],[31,53],[31,57],[40,41],[6,7],[22,34],[7,12],[21,38],[32,37],[35,38],[40,45]],[[44,58],[28,41],[52,63],[27,29],[53,54],[45,47],[32,39],[18,21],[36,38],[0,24],[8,39],[28,34],[46,48],[48,51],[16,19],[48,51],[3,34],[6,42],[40,47],[25,31],[23,48],[48,58],[46,57],[3,6],[40,44],[13,15],[12,31],[24,26],[0,3],[39,62],[41,44],[25,46]],[[10,12],[25,28],[22,36],[5,52],[20,52],[60,62],[37,59],[14,46],[45,57],[28,31],[40,41],[12,21],[52,53],[14,15],[13,55],[18,27],[6,7],[50,55],[26,27],[27,31],[1,2],[17,19],[12,16],[50,53],[20,40],[52,63],[1,26],[59,63],[2,4],[8,13],[42,47],[50,55]],[[18,20],[14,45],[4,44],[48,51],[32,57],[13,58],[11,13],[18,20],[13,61],[1,12],[58,59],[44,47],[16,19],[0,5],[45,46],[1,5],[35,37],[33,37],[10,22],[0,2],[13,18],[1,62],[27,30],[3,6],[8,10],[22,23],[7,47],[34,37],[22,23],[0,7],[51,61],[22,49]],[[5,45],[61,62],[35,39],[12,21],[1,19],[21,44],[7,47],[13,52],[9,13],[26,58],[61,62],[40,41],[34,38],[17,18],[57,61],[57,62],[22,50],[59,63],[4,14],[10,14],[58,63],[1,56],[60,62],[12,59],[26,47],[11,13],[18,53],[45,62],[26,38],[26,33],[33,37],[5,46]],[[46,47],[33,43],[45,46],[0,5],[24,30],[26,34],[45,59],[1,5],[18,63],[7,52],[31,34],[57,60],[34,57],[28,29],[24,42],[16,21],[48,54],[10,13],[22,43],[48,52],[61,62],[18,22],[25,40],[2,4],[58,61],[51,52],[12,32],[6,61],[39,52],[42,43],[2,42],[19,21]],[[5,6],[16,22],[45,57],[2,3],[9,32],[17,23],[13,49],[36,61],[2,3],[41,44],[41,42],[9,13],[6,13],[0,3],[23,62],[24,25],[54,55],[26,31],[14,31],[23,49],[58,60],[31,42],[18,20],[3,40],[29,30],[8,21],[33,49],[10,14],[8,11],[1,3],[32,37],[17,22]],[[7,21],[11,31],[44,46],[51,53],[44,57],[27,31],[40,41],[2,52],[33,40],[8,24],[10,60],[35,36],[42,46],[7,21],[26,60],[35,61],[54,63],[9,10],[30,61],[44,51],[11,13],[1,35],[1,12],[58,62],[56,62],[42,47],[54,63],[51,54],[2,5],[44,56],[9,25],[25,28]],[[9,11],[1,30],[26,30],[56,60],[18,19],[3,51],[33,62],[6,7],[42,45],[9,10],[29,48],[38,57],[33,50],[41,42],[17,22],[48,59],[24,27],[27,29],[7,57],[46,54],[36,38],[51,53],[14,56],[3,7],[2,6],[7,52],[26,31],[36,42],[8,37],[37,38],[6,34],[50,54]],[[42,45],[34,37],[10,13],[33,37],[8,28],[12,38],[56,60],[3,56],[17,47],[4,7],[11,13],[43,45],[22,23],[22,28],[5,7],[51,61],[11,59],[62,63],[7,15],[7,54],[7,55],[57,62],[9,10],[20,39],[37,51],[57,58],[40,61],[12,13],[59,61],[10,14],[15,62],[27,55]]]
CAP = 79
def setup_inputs(rng):
    return {"x": rng.standard_normal((N, TOK, D), dtype=np.float32)}
def reference(x):
    y = np.full((N, CAP, D), np.nan, x.dtype)
    fill = [0] * N
    for r in range(N):
        for t in range(TOK):
            for e in ROUTE[r][t]:
                if fill[e] < CAP:
                    y[e][fill[e]] = x[r][t]
                    fill[e] += 1
    return {"y": y}

@@ -1,0 +1,270 @@
+import concourse.bass as bass
+import comms_topo as ct
+
+SCRATCH = {
+    "stage": ("dram", [32, 128, 4], "float32"),
+    "land": ("dram", [79, 128, 4], "float32"),
+}
+SEMAPHORES = ["loaded", "kept", "sent", "arr1", "arr2", "arr3", "stored"]
+
+TARGET = {"cout": 55.0, "swi": 140.0, "swo": 125.0, "mate": 80.0}
+POWER = 12
+ROUNDS = 5
+CALL_LIMIT = {"t2": 16, "f2": 8, "t3": 16, "f3": 8}
+PORT_CORES = (2, 3, 6, 7)
+PLAN = {}
+MEMO = {}
+
+
+def gchip(c):
+    return c // 8
+
+
+def edge_res(w, d):
+    key = (w, d)
+    if key in MEMO:
+        return MEMO[key]
+    res = [("cout", w), ("cin", d)]
+    cw, cd = gchip(w), gchip(d)
+    if cw != cd:
+        res.append(("chout", cw))
+        die = ct.die(w)
+        cur = cw
+        if (cw ^ cd) & 1:
+            res.append(("mate", cw * 2 + die))
+            cur = cw ^ 1
+        if cur != cd:
+            res.append(("swo", cur * 2 + die))
+            res.append(("swi", cd * 2 + die))
+    MEMO[key] = res
+    return res
+
+
+def make_plan(cores, route, cap, ncores=256):
+    n = len(cores)
+    group = set(cores)
+    gchips = set(gchip(c) for c in cores)
+    idle = [c for c in range(ncores) if gchip(c) not in gchips]
+    cnt = [0] * n
+    need_in = {c: 0 for c in cores}
+    selfs = {c: 0 for c in cores}
+    toks = []
+    rows = []
+    must_leave = {}
+    for r in range(n):
+        for t in range(len(route[r])):
+            s = cores[r]
+            ds = []
+            rw = {}
+            for e in route[r][t]:
+                rw[cores[e]] = cnt[e]
+                cnt[e] += 1
+                if e != r:
+                    need_in[cores[e]] += 1
+                    ds.append(cores[e])
+                else:
+                    selfs[s] += 1
+            toks.append((s, tuple(ds)))
+            rows.append((t, rw))
+            if any(gchip(d) != gchip(s) for d in ds):
+                must_leave[gchip(s)] = must_leave.get(gchip(s), 0) + 1
+    cin_cap = max(need_in.values())
+    chout_cap = max(must_leave.values())
+    load = {}
+
+    def tree_res(tree):
+        delta = {}
+        calls = {}
+        for (w, d, dep) in tree:
+            for ki in edge_res(w, d):
+                delta[ki] = delta.get(ki, 0) + 1
+            if dep > 1 and w in group:
+                calls[(w, dep)] = calls.get((w, dep), False) or gchip(w) != gchip(d)
+        for (w, dep), far in calls.items():
+            delta[("t%d" % dep, w)] = 1
+            if far:
+                delta[("f%d" % dep, w)] = 1
+        return delta
+
+    def add(tree, sgn):
+        for ki, dl in tree_res(tree).items():
+            load[ki] = load.get(ki, 0) + sgn * dl
+
+    def cost(tree, strict, s, ds):
+        c = 1e-3 * len(tree)
+        for ki, dl in tree_res(tree).items():
+            k, i = ki
+            l = load.get(ki, 0)
+            if k == "cin":
+                if l + dl > cin_cap or l + dl + selfs.get(i, 0) > cap:
+                    return None
+                if strict and i in group and i not in ds:
+                    return None
+            elif k == "chout":
+                if l + dl > chout_cap:
+                    return None
+                if strict and i in gchips and (i != gchip(s) or dl > 1):
+                    return None
+            elif k in CALL_LIMIT:
+                if l + dl > CALL_LIMIT[k]:
+                    c += 1000.0
+            if k in TARGET:
+                tk = TARGET[k]
+                c += ((l + dl) / tk) ** POWER - (l / tk) ** POWER + 1e-6 * dl * (l + 1)
+        return c
+
+    def valid(s, ds, tree):
+        ent = {}
+        hx = 0
+        for (w, d, dep) in tree:
+            if w == d or not ct.may_write(w, d):
+                return False
+            cw, cd = gchip(w), gchip(d)
+            if cw != cd:
+                if cd in gchips:
+                    ent[cd] = ent.get(cd, 0) + 1
+                if cw // 16 != cd // 16:
+                    hx += 1
+        need = set(gchip(d) for d in ds if gchip(d) != gchip(s))
+        if set(ent) != need or any(v > 1 for v in ent.values()):
+            return False
+        return hx == (1 if any(d // 128 != s // 128 for d in ds) else 0)
+
+    def relays(s, ds):
+        out = [g for g in range(gchip(s) * 8, gchip(s) * 8 + 8) if g != s and g % 8 in PORT_CORES and g not in ds]
+        best = {}
+        for g in idle:
+            if (gchip(g) ^ gchip(s)) & 1:
+                continue
+            key = (gchip(g), ct.die(g), g % 8 in PORT_CORES)
+            l = load.get(("cin", g), 0) + load.get(("cout", g), 0)
+            if key not in best or l < best[key][0]:
+                best[key] = (l, g)
+        out += [best[k][1] for k in sorted(best)]
+        return out
+
+    def candidates(s, ds):
+        c = []
+        if len(ds) == 1:
+            d = ds[0]
+            c.append([(s, d, 1)])
+            if not ct.may_write(s, d):
+                for g in relays(s, ds):
+                    c.append([(s, g, 1), (g, d, 2)])
+        else:
+            a, b = ds
+            c.append([(s, a, 1), (s, b, 1)])
+            c.append([(s, a, 1), (a, b, 2)])
+            c.append([(s, b, 1), (b, a, 2)])
+            ca, cb, cs = gchip(a), gchip(b), gchip(s)
+            if not (ct.may_write(s, a) and ct.may_write(s, b)) or (ca != cb and ca != cs and cb != cs):
+                for g in relays(s, ds):
+                    if ca != cb:
+                        c.append([(s, g, 1), (g, a, 2), (g, b, 2)])
+                        c.append([(s, a, 1), (s, g, 1), (g, b, 2)])
+                        c.append([(s, b, 1), (s, g, 1), (g, a, 2)])
+                    if ca == cb or ca == cb ^ 1:
+                        c.append([(s, g, 1), (g, a, 2), (a, b, 3)])
+                        c.append([(s, g, 1), (g, b, 2), (b, a, 3)])
+        return [x for x in c if valid(s, ds, x)]
+
+    chosen = [None] * len(toks)
+    for rd in range(ROUNDS):
+        for i, (s, ds) in enumerate(toks):
+            if chosen[i] is not None:
+                add(chosen[i], -1)
+            best = None
+            for tr in candidates(s, ds):
+                cc = cost(tr, rd == 0, s, ds)
+                if cc is not None and (best is None or cc < best[0]):
+                    best = (cc, tr)
+            chosen[i] = best[1]
+            add(best[1], 1)
+
+    free = {c: 0 for c in range(ncores)}
+    for r in range(n):
+        free[cores[r]] = cnt[r]
+    sends = {c: {1: [], 2: [], 3: []} for c in range(ncores)}
+    arrive = {c: {1: 0, 2: 0, 3: 0} for c in range(ncores)}
+    keep = {c: [] for c in range(ncores)}
+    for i, (s, ds) in enumerate(toks):
+        t, rw = rows[i]
+        if s in rw:
+            keep[s].append((t, rw[s]))
+        place = {s: ("stage", t)}
+        for (w, d, dep) in chosen[i]:
+            if d in rw:
+                place[d] = ("land", rw[d])
+            else:
+                place[d] = ("land", free[d])
+                free[d] += 1
+            arrive[d][dep] += 1
+        by = {}
+        for (w, d, dep) in chosen[i]:
+            by.setdefault((w, dep), []).append((d, place[d][1]))
+        for (w, dep) in sorted(by):
+            sends[w][dep].append((place[w][0], place[w][1], by[(w, dep)]))
+    return {"sends": sends, "arrive": arrive, "keep": keep, "cnt": cnt}
+
+
+def emit(g, core, T, topo, transfers, sem):
+    far = [x for x in transfers if any(gchip(d) != gchip(core) for (d, k) in x[2])]
+    near = [x for x in transfers if not any(gchip(d) != gchip(core) for (d, k) in x[2])]
+    while far or near:
+        batch = []
+        while far and len(batch) < 8:
+            batch.append(far.pop(0))
+        while near and len(batch) < 16:
+            batch.append(near.pop(0))
+        trs = []
+        for eng, (buf, slot, dsts) in enumerate(batch):
+            src = T.stage[slot] if buf == "stage" else T.land[slot]
+            ids = []
+            for (d, k) in dsts:
+                rid, pid = topo.addr(d, core)
+                ids.append(bass.DstId(rid=rid, pnc=pid))
+            trs.append(bass.RemoteDMATransfer(dst_ids=ids, dma_engine_mask=1 << eng, remote_sem=sem,
+                                              srcs=[src], dsts=[T.land[k] for (d, k) in dsts]))
+        g.remote_dma_fused(trs, local_sem=T.sem.sent)
+    return len(transfers)
+
+
+def rank_program(g, core, T, topo):
+    if "p" not in PLAN:
+        PLAN["p"] = make_plan(list(T.cores), T.tables["ROUTE"], T.tables["CAP"])
+    p = PLAN["p"]
+    rank = T.rank_of(core)
+    sends, arrive, keep = p["sends"][core], p["arrive"][core], p["keep"][core]
+    sems = {1: T.sem.arr1, 2: T.sem.arr2, 3: T.sem.arr3}
+    nkept = 0
+    if rank is not None:
+        g.dma_start(T.stage[:], T.x[:]).then_inc(T.sem.loaded, 16)
+        j = 0
+        while j < len(keep):
+            m = 1
+            if j + 1 < len(keep):
+                step = keep[j + 1][0] - keep[j][0]
+                m = 2
+                while j + m < len(keep) and keep[j + m][0] - keep[j + m - 1][0] == step:
+                    m += 1
+            t0, row = keep[j]
+            if m == 1:
+                g.dma_start(T.land[row], T.x[t0]).then_inc(T.sem.kept, 16)
+            else:
+                g.dma_start(T.land[row:row + m], T.x[t0:t0 + (m - 1) * step + 1:step]).then_inc(T.sem.kept, 16)
+            nkept += 16
+            j += m
+        g.wait_ge(T.sem.loaded, 16)
+    nsent = 0
+    for dep in (1, 2, 3):
+        nsent += emit(g, core, T, topo, sends[dep], sems[dep])
+        if arrive[dep]:
+            g.wait_ge(sems[dep], arrive[dep])
+    if rank is not None:
+        if nkept:
+            g.wait_ge(T.sem.kept, nkept)
+        c = p["cnt"][rank]
+        g.dma_start(T.y[0:c], T.land[0:c]).then_inc(T.sem.stored, 16)
+        g.wait_ge(T.sem.stored, 16)
+    if nsent:
+        g.wait_ge(T.sem.sent, nsent)

@@ -1,3 +1,4 @@
+import math
 import concourse.bass as bass
 import comms_topo as ct
 
@@ -9,8 +10,8 @@ SEMAPHORES = ["loaded", "kept", "sent", "arr1", "arr2", "arr3", "stored"]
 
 TARGET = {"cout": 55.0, "swi": 140.0, "swo": 125.0, "mate": 80.0}
 POWER = 12
-ROUNDS = 5
-CALL_LIMIT = {"t2": 16, "f2": 8, "t3": 16, "f3": 8}
+ROUNDS = 4
+CALL_LIMIT = {"t2": 16, "f2": 8, "t3": 16}
 PORT_CORES = (2, 3, 6, 7)
 PLAN = {}
 MEMO = {}
@@ -163,14 +164,18 @@ def make_plan(cores, route, cap, ncores=256):
                         c.append([(s, g, 1), (g, a, 2), (g, b, 2)])
                         c.append([(s, a, 1), (s, g, 1), (g, b, 2)])
                         c.append([(s, b, 1), (s, g, 1), (g, a, 2)])
-                    if ca == cb or ca == cb ^ 1:
+                    else:
                         c.append([(s, g, 1), (g, a, 2), (a, b, 3)])
                         c.append([(s, g, 1), (g, b, 2), (b, a, 3)])
         return [x for x in c if valid(s, ds, x)]
 
     chosen = [None] * len(toks)
+    stride = 37
+    while math.gcd(stride, len(toks)) != 1:
+        stride += 1
     for rd in range(ROUNDS):
-        for i, (s, ds) in enumerate(toks):
+        for i in [(j * stride) % len(toks) for j in range(len(toks))]:
+            s, ds = toks[i]
             if chosen[i] is not None:
                 add(chosen[i], -1)
             best = None

import math
import concourse.bass as bass
import comms_topo as ct

SCRATCH = {
    "stage": ("dram", [32, 128, 4], "float32"),
    "land": ("dram", [79, 128, 4], "float32"),
}
SEMAPHORES = ["loaded", "kept", "sent", "arr1", "arr2", "arr3", "stored"]

TARGET = {"cout": 55.0, "swi": 140.0, "swo": 125.0, "mate": 80.0}
POWER = 12
ROUNDS = 4
CALL_LIMIT = {"t2": 16, "f2": 8, "t3": 16}
PORT_CORES = (2, 3, 6, 7)
PLAN = {}
MEMO = {}


def gchip(c):
    return c // 8


def edge_res(w, d):
    key = (w, d)
    if key in MEMO:
        return MEMO[key]
    res = [("cout", w), ("cin", d)]
    cw, cd = gchip(w), gchip(d)
    if cw != cd:
        res.append(("chout", cw))
        die = ct.die(w)
        cur = cw
        if (cw ^ cd) & 1:
            res.append(("mate", cw * 2 + die))
            cur = cw ^ 1
        if cur != cd:
            res.append(("swo", cur * 2 + die))
            res.append(("swi", cd * 2 + die))
    MEMO[key] = res
    return res


def make_plan(cores, route, cap, ncores=256):
    n = len(cores)
    group = set(cores)
    gchips = set(gchip(c) for c in cores)
    idle = [c for c in range(ncores) if gchip(c) not in gchips]
    cnt = [0] * n
    need_in = {c: 0 for c in cores}
    selfs = {c: 0 for c in cores}
    toks = []
    rows = []
    must_leave = {}
    for r in range(n):
        for t in range(len(route[r])):
            s = cores[r]
            ds = []
            rw = {}
            for e in route[r][t]:
                rw[cores[e]] = cnt[e]
                cnt[e] += 1
                if e != r:
                    need_in[cores[e]] += 1
                    ds.append(cores[e])
                else:
                    selfs[s] += 1
            toks.append((s, tuple(ds)))
            rows.append((t, rw))
            if any(gchip(d) != gchip(s) for d in ds):
                must_leave[gchip(s)] = must_leave.get(gchip(s), 0) + 1
    cin_cap = max(need_in.values())
    chout_cap = max(must_leave.values())
    load = {}

    def tree_res(tree):
        delta = {}
        calls = {}
        for (w, d, dep) in tree:
            for ki in edge_res(w, d):
                delta[ki] = delta.get(ki, 0) + 1
            if dep > 1 and w in group:
                calls[(w, dep)] = calls.get((w, dep), False) or gchip(w) != gchip(d)
        for (w, dep), far in calls.items():
            delta[("t%d" % dep, w)] = 1
            if far:
                delta[("f%d" % dep, w)] = 1
        return delta

    def add(tree, sgn):
        for ki, dl in tree_res(tree).items():
            load[ki] = load.get(ki, 0) + sgn * dl

    def cost(tree, strict, s, ds):
        c = 1e-3 * len(tree)
        for ki, dl in tree_res(tree).items():
            k, i = ki
            l = load.get(ki, 0)
            if k == "cin":
                if l + dl > cin_cap or l + dl + selfs.get(i, 0) > cap:
                    return None
                if strict and i in group and i not in ds:
                    return None
            elif k == "chout":
                if l + dl > chout_cap:
                    return None
                if strict and i in gchips and (i != gchip(s) or dl > 1):
                    return None
            elif k in CALL_LIMIT:
                if l + dl > CALL_LIMIT[k]:
                    c += 1000.0
            if k in TARGET:
                tk = TARGET[k]
                c += ((l + dl) / tk) ** POWER - (l / tk) ** POWER + 1e-6 * dl * (l + 1)
        return c

    def valid(s, ds, tree):
        ent = {}
        hx = 0
        for (w, d, dep) in tree:
            if w == d or not ct.may_write(w, d):
                return False
            cw, cd = gchip(w), gchip(d)
            if cw != cd:
                if cd in gchips:
                    ent[cd] = ent.get(cd, 0) + 1
                if cw // 16 != cd // 16:
                    hx += 1
        need = set(gchip(d) for d in ds if gchip(d) != gchip(s))
        if set(ent) != need or any(v > 1 for v in ent.values()):
            return False
        return hx == (1 if any(d // 128 != s // 128 for d in ds) else 0)

    def relays(s, ds):
        out = [g for g in range(gchip(s) * 8, gchip(s) * 8 + 8) if g != s and g % 8 in PORT_CORES and g not in ds]
        best = {}
        for g in idle:
            if (gchip(g) ^ gchip(s)) & 1:
                continue
            key = (gchip(g), ct.die(g), g % 8 in PORT_CORES)
            l = load.get(("cin", g), 0) + load.get(("cout", g), 0)
            if key not in best or l < best[key][0]:
                best[key] = (l, g)
        out += [best[k][1] for k in sorted(best)]
        return out

    def candidates(s, ds):
        c = []
        if len(ds) == 1:
            d = ds[0]
            c.append([(s, d, 1)])
            if not ct.may_write(s, d):
                for g in relays(s, ds):
                    c.append([(s, g, 1), (g, d, 2)])
        else:
            a, b = ds
            c.append([(s, a, 1), (s, b, 1)])
            c.append([(s, a, 1), (a, b, 2)])
            c.append([(s, b, 1), (b, a, 2)])
            ca, cb, cs = gchip(a), gchip(b), gchip(s)
            if not (ct.may_write(s, a) and ct.may_write(s, b)) or (ca != cb and ca != cs and cb != cs):
                for g in relays(s, ds):
                    if ca != cb:
                        c.append([(s, g, 1), (g, a, 2), (g, b, 2)])
                        c.append([(s, a, 1), (s, g, 1), (g, b, 2)])
                        c.append([(s, b, 1), (s, g, 1), (g, a, 2)])
                    else:
                        c.append([(s, g, 1), (g, a, 2), (a, b, 3)])
                        c.append([(s, g, 1), (g, b, 2), (b, a, 3)])
        return [x for x in c if valid(s, ds, x)]

    chosen = [None] * len(toks)
    stride = 37
    while math.gcd(stride, len(toks)) != 1:
        stride += 1
    for rd in range(ROUNDS):
        for i in [(j * stride) % len(toks) for j in range(len(toks))]:
            s, ds = toks[i]
            if chosen[i] is not None:
                add(chosen[i], -1)
            best = None
            for tr in candidates(s, ds):
                cc = cost(tr, rd == 0, s, ds)
                if cc is not None and (best is None or cc < best[0]):
                    best = (cc, tr)
            chosen[i] = best[1]
            add(best[1], 1)

    free = {c: 0 for c in range(ncores)}
    for r in range(n):
        free[cores[r]] = cnt[r]
    sends = {c: {1: [], 2: [], 3: []} for c in range(ncores)}
    arrive = {c: {1: 0, 2: 0, 3: 0} for c in range(ncores)}
    keep = {c: [] for c in range(ncores)}
    for i, (s, ds) in enumerate(toks):
        t, rw = rows[i]
        if s in rw:
            keep[s].append((t, rw[s]))
        place = {s: ("stage", t)}
        for (w, d, dep) in chosen[i]:
            if d in rw:
                place[d] = ("land", rw[d])
            else:
                place[d] = ("land", free[d])
                free[d] += 1
            arrive[d][dep] += 1
        by = {}
        for (w, d, dep) in chosen[i]:
            by.setdefault((w, dep), []).append((d, place[d][1]))
        for (w, dep) in sorted(by):
            sends[w][dep].append((place[w][0], place[w][1], by[(w, dep)]))
    return {"sends": sends, "arrive": arrive, "keep": keep, "cnt": cnt}


def emit(g, core, T, topo, transfers, sem):
    far = [x for x in transfers if any(gchip(d) != gchip(core) for (d, k) in x[2])]
    near = [x for x in transfers if not any(gchip(d) != gchip(core) for (d, k) in x[2])]
    while far or near:
        batch = []
        while far and len(batch) < 8:
            batch.append(far.pop(0))
        while near and len(batch) < 16:
            batch.append(near.pop(0))
        trs = []
        for eng, (buf, slot, dsts) in enumerate(batch):
            src = T.stage[slot] if buf == "stage" else T.land[slot]
            ids = []
            for (d, k) in dsts:
                rid, pid = topo.addr(d, core)
                ids.append(bass.DstId(rid=rid, pnc=pid))
            trs.append(bass.RemoteDMATransfer(dst_ids=ids, dma_engine_mask=1 << eng, remote_sem=sem,
                                              srcs=[src], dsts=[T.land[k] for (d, k) in dsts]))
        g.remote_dma_fused(trs, local_sem=T.sem.sent)
    return len(transfers)


def rank_program(g, core, T, topo):
    if "p" not in PLAN:
        PLAN["p"] = make_plan(list(T.cores), T.tables["ROUTE"], T.tables["CAP"])
    p = PLAN["p"]
    rank = T.rank_of(core)
    sends, arrive, keep = p["sends"][core], p["arrive"][core], p["keep"][core]
    sems = {1: T.sem.arr1, 2: T.sem.arr2, 3: T.sem.arr3}
    nkept = 0
    if rank is not None:
        g.dma_start(T.stage[:], T.x[:]).then_inc(T.sem.loaded, 16)
        j = 0
        while j < len(keep):
            m = 1
            if j + 1 < len(keep):
                step = keep[j + 1][0] - keep[j][0]
                m = 2
                while j + m < len(keep) and keep[j + m][0] - keep[j + m - 1][0] == step:
                    m += 1
            t0, row = keep[j]
            if m == 1:
                g.dma_start(T.land[row], T.x[t0]).then_inc(T.sem.kept, 16)
            else:
                g.dma_start(T.land[row:row + m], T.x[t0:t0 + (m - 1) * step + 1:step]).then_inc(T.sem.kept, 16)
            nkept += 16
            j += m
        g.wait_ge(T.sem.loaded, 16)
    nsent = 0
    for dep in (1, 2, 3):
        nsent += emit(g, core, T, topo, sends[dep], sems[dep])
        if arrive[dep]:
            g.wait_ge(sems[dep], arrive[dep])
    if rank is not None:
        if nkept:
            g.wait_ge(T.sem.kept, nkept)
        c = p["cnt"][rank]
        g.dma_start(T.y[0:c], T.land[0:c]).then_inc(T.sem.stored, 16)
        g.wait_ge(T.sem.stored, 16)
    if nsent:
        g.wait_ge(T.sem.sent, nsent)
